import numpy as np, ml_dtypes
CORES = [3,7,11,15,131,135,139,143]
N = 8
import mx_ref
NC, G, NE = 256, 4, 128
C = np.float32(0.023)
EX = [0,0,0,0,1,1,1,1]
BF = ml_dtypes.bfloat16
def cut(t, i, w=512):
    return t[:, w * i:w * i + w]
def tile(rs):
    return np.stack(rs, axis=2).reshape(128, -1).astype(BF)
def layer(w, X):
    out = []
    for i in range(G):
        for t in range(len(X)):
            p = mx_ref.matmul(mx_ref.quantize(cut(w, len(X) * i + t)), X[t])
            z = p if t == 0 else z + p
        out.append(z)
    return out
def act(Z):
    return [np.maximum(z, 0) * C for z in Z]
def setup_inputs(rng):
    def f(*shape):
        return mx_ref.flush((rng.standard_normal(shape, dtype=np.float32) * np.exp2(rng.integers(-2, 3, shape[:-1] + (1,)))).astype(BF))
    return {"x": f(N, 128, 4 * NC), "w1": f(N, 128, G * 512), "w2": f(N, 128, 512)}
def setup_inputs_blocks(rng):
    d = setup_inputs(rng)
    for k in ("x", "w1", "w2"): d[k] = mx_ref.spread(d[k], rng, 2)
    return d
def setup_inputs_wide(rng):
    d = setup_inputs(rng)
    for k in ("x", "w1", "w2"): d[k] = mx_ref.flush((d[k].astype(np.float32) * np.exp2(rng.integers(-6, 7, (N, 1, 1))).astype(np.float32)).astype(BF))
    return d
def reference(x, w1, w2):
    y = np.zeros((N, 128, NC), np.float32)
    for j in range(N):
        for e in range(2):
            X = mx_ref.quantize(cut(x[j], e, 4 * NE)); z = None
            for r in [r_ for r_ in range(N) if EX[r_] == e]:
                p = mx_ref.matmul(mx_ref.quantize(w2[r]), mx_ref.quantize(tile(act(layer(w1[r], [X])))))
                z = p if z is None else z + p
            y[j][:, NE * e:NE * e + NE] = z
    return {"y": y}

@@ -1,0 +1,323 @@
+from concourse.bass import DstId, RemoteDMATransfer
+from concourse.mybir import dt, AluOpType, ActivationFunctionType
+
+CFG = dict(wpair="chip", swap=0, fwde="lo", oute="lo", cpA="s", acteng="svsv",
+           ldsync="x' w1 w2 x", ldscalar="", vq="x' w1 w2 x",
+           gs="xc xs wc:hi ws:lo oc os fc fs",
+           ts="u1 u3 A0 u4 u9 A1 u2 M0 u10 K0 M1 u5 K1 HC u6 C0 C1 S HB")
+
+SCRATCH = {
+    "xin": ("sbuf", [128, 1024], "bfloat16"),
+    "w1in": ("sbuf", [128, 2048], "bfloat16"),
+    "w2in": ("sbuf", [128, 512], "bfloat16"),
+    "xs": ("sbuf", [128, 128], "float8_e4m3fn_x4"),
+    "xsp": ("sbuf", [128, 128], "uint8"),
+    "xm": ("sbuf", [128, 512], "float8_e4m3fn_x4"),
+    "xmp": ("sbuf", [128, 512], "uint8"),
+    "wq": ("sbuf", [128, 1280], "float8_e4m3fn_x4"),
+    "wp": ("sbuf", [128, 1280], "uint8"),
+    "h": ("sbuf", [128, 4096], "bfloat16"),
+    "hq": ("sbuf", [128, 1024], "float8_e4m3fn_x4"),
+    "hp": ("sbuf", [128, 1024], "uint8"),
+    "ypart": ("sbuf", [128, 128], "float32"),
+    "ysum": ("sbuf", [128, 128], "float32"),
+    "yhome": ("sbuf", [128, 128], "float32"),
+    "yown": ("sbuf", [128, 128], "float32"),
+    "lpart": ("sbuf", [128, 128], "float32"),
+    "lhome": ("sbuf", [128, 128], "float32"),
+    "lfar": ("sbuf", [128, 128], "float32"),
+    "z": ("psum", [128, 2560], "float32"),
+    "yps": ("psum", [128, 1536], "float32"),
+}
+SEMAPHORES = ["ldx0", "ldx1", "ldwa", "ldwb", "ldw2", "st0", "st1", "vt", "vs", "vv", "sent",
+              "a_c", "a_s", "f_c", "f_s", "o_c", "o_s", "w_c", "w_c2", "w_s", "r_part", "r_home", "r_far"]
+
+
+def rank_program(g, core, T, topo):
+    rank = T.rank_of(core)
+    if rank is None:
+        return
+    S = T.sem
+    e = T.tables["EX"][rank]
+
+    def chipmate(a):
+        return [k for k in T.cores if k != a and topo.host(a) == topo.host(k) and topo.chip(a) == topo.chip(k)][0]
+
+    def matemate(a):
+        return [k for k in T.cores if topo.mates(a, k) and topo.die(a) == topo.die(k)][0]
+
+    def across(a):
+        return [k for k in T.cores if topo.host(k) != topo.host(a) and topo.chip(k) == topo.chip(a) and topo.die(k) == topo.die(a)][0]
+
+    wpair, xpair = (chipmate, matemate) if CFG["wpair"] == "chip" else (matemate, chipmate)
+    b, c = wpair(core), xpair(core)
+    far = across(core)
+    far_in, far_out = (xpair(far), far) if CFG["swap"] else (far, xpair(far))
+
+    def engines(dst):
+        m = topo.mask(core, dst)
+        return [k for k in range(m.bit_length()) if m >> k & 1]
+
+    lo = engines(far)
+    allc = engines(chipmate(core))
+    hi = [k for k in allc if k not in lo]
+
+    def pick(dst, which):
+        ok = engines(dst)
+        n = len(lo) // 2
+        want = {"lo": lo, "hi": hi, "all": allc, "lo4": lo[:n], "lh4": lo[n:], "hi4": hi[:n], "hh4": hi[n:]}[which or "lo"]
+        return [k for k in want if k in ok] or ok
+
+    def bits(l):
+        return sum(1 << k for k in l)
+
+    def ap(buf, a, n):
+        return T[buf][:, a:a + n]
+
+    def sides(obuf, oc, ibuf, ic, n, code):
+        o, i = ap(obuf, oc, n), ap(ibuf, ic, n)
+        return (o.bitcast(dt.uint8), i.bitcast(dt.uint8)) if code else (o, i)
+
+    sent = [0]
+    arr = {}
+
+    def send(dst, obuf, oc, ibuf, ic, n, sem, eng, code=False):
+        rid, pid = topo.addr(dst, core)
+        o, i = sides(obuf, oc, ibuf, ic, n, code)
+        sent[0] += len(eng)
+        arr[sem] = len(eng)
+        g.remote_dma(out_ap=o, in_ap=i, remote_sem=S[sem], local_sem=S["sent"], pid=pid, routing_id=rid, dma_engine_mask=bits(eng))
+
+    def fused(l):
+        trs = []
+        for dst, obuf, oc, ibuf, ic, n, sem, eng, code in l:
+            rid, pid = topo.addr(dst, core)
+            o, i = sides(obuf, oc, ibuf, ic, n, code)
+            sent[0] += len(eng)
+            arr[sem] = len(eng)
+            trs.append(RemoteDMATransfer(dst_ids=[DstId(rid=rid, pnc=pid)], dma_engine_mask=bits(eng), remote_sem=S[sem], src=i, dst=o))
+        g.remote_dma_fused(trs, local_sem=S["sent"])
+
+    V = g.vector
+    q = g.tensor
+    qsem = {"t": "vt", "s": "vs", "v": "vv"}
+    done = {"t": 0, "s": 0, "v": 0}
+    known = {}
+    seen = {}
+
+    def mark(qn, inst):
+        done[qn] += 1
+        inst.then_inc(S[qsem[qn]], 1)
+        return (qn, done[qn])
+
+    def need(qn, queue, toks):
+        m = {}
+        for t in toks:
+            m[t[0]] = max(m.get(t[0], 0), t[1])
+        for s, v in m.items():
+            if known.get((qn, s), 0) < v:
+                queue.wait_ge(S[qsem[s]], v)
+                known[qn, s] = v
+
+    def land(qn, queue, sem, n):
+        if seen.get((qn, sem), 0) < n:
+            queue.wait_ge(S[sem], n)
+            seen[qn, sem] = n
+
+    own0, rem0 = 512 * e, 512 * (1 - e)
+    LD = {"x'": ("xin", "x", rem0, 512, "ldx0"), "x": ("xin", "x", own0, 512, "ldx1"),
+          "wa": ("w1in", "w1", 0, 1024, "ldwa"), "wb": ("w1in", "w1", 1024, 1024, "ldwb"),
+          "w1": ("w1in", "w1", 0, 2048, "ldwa"), "w2": ("w2in", "w2", 0, 512, "ldw2")}
+    for queue, names in ((g.sync, CFG["ldsync"]), (g.scalar, CFG["ldscalar"])):
+        for nm in names.split():
+            o, i, c0, n, sm = LD[nm]
+            queue.dma_start(T[o][:, c0:c0 + n], T[i][:, c0:c0 + n]).then_inc(S[sm], 16)
+
+    def quant(out, oc, pl, src, sc, n):
+        return mark("v", V.quantize_mx(ap(out, oc, n), ap(pl, oc, n), ap(src, sc, 4 * n)))
+
+    tk = {}
+    for nm in CFG["vq"].split():
+        land("v", V, LD[nm][4], 16)
+        if nm == "x'":
+            tk["xr"] = quant("xs", 0, "xsp", "xin", rem0, 128)
+        if nm == "x":
+            tk["xo"] = quant("xm", 384, "xmp", "xin", own0, 128)
+        if nm == "wa":
+            tk["wa"] = quant("wq", 0, "wp", "w1in", 0, 256)
+        if nm == "wb":
+            tk["wb"] = quant("wq", 256, "wp", "w1in", 1024, 256)
+        if nm == "w1":
+            tk["wa"] = tk["wb"] = quant("wq", 0, "wp", "w1in", 0, 512)
+        if nm == "w2":
+            tk["w2"] = quant("wq", 512, "wp", "w2in", 0, 128)
+
+    wsem = []
+    allw = [tk["wa"], tk["wb"], tk["w2"]]
+    for nm in CFG["gs"].split():
+        nm, _, ee = nm.partition(":")
+        es = ee.split("+")
+        if nm == "xc":
+            need("g", g, [tk["xr"]])
+            send(far_in, "xm", 0, "xs", 0, 128, "a_c", pick(far_in, ee), True)
+        if nm == "xs":
+            need("g", g, [tk["xr"]])
+            send(far_in, "xmp", 0, "xsp", 0, 128, "a_s", pick(far_in, ee))
+        if nm == "xs2":
+            need("g", g, [tk["xr"]])
+            fused([(far_in, "xmp", 0, "xsp", 0, 128, "a_s", pick(far_in, es[0]), False),
+                   (far_out, "xmp", 128, "xsp", 0, 128, "f_s", pick(far_out, es[1]), False)])
+        if nm == "oc":
+            need("g", g, [tk["xo"]])
+            send(c, "xm", 256, "xm", 384, 128, "o_c", pick(c, ee), True)
+        if nm == "os":
+            need("g", g, [tk["xo"]])
+            send(c, "xmp", 256, "xmp", 384, 128, "o_s", pick(c, ee))
+        if nm == "fxc":
+            need("g", g, [tk["xr"], tk["xo"]])
+            fused([(far_in, "xm", 0, "xs", 0, 128, "a_c", pick(far_in, es[0]), True),
+                   (c, "xm", 256, "xm", 384, 128, "o_c", pick(c, es[1]), True)])
+        if nm in ("fxs", "fx3"):
+            need("g", g, [tk["xr"], tk["xo"]])
+            fused([(far_in, "xmp", 0, "xsp", 0, 128, "a_s", pick(far_in, es[0]), False),
+                   (c, "xmp", 256, "xmp", 384, 128, "o_s", pick(c, es[1]), False)]
+                  + ([(far_out, "xmp", 128, "xsp", 0, 128, "f_s", pick(far_out, es[2]), False)] if nm == "fx3" else []))
+        if nm == "wc":
+            need("g", g, allw)
+            send(b, "wq", 640, "wq", 0, 640, "w_c", pick(b, ee), True)
+            wsem.append("w_c")
+        if nm == "wc1":
+            need("g", g, [tk["wa"]])
+            send(b, "wq", 640, "wq", 0, 256, "w_c", pick(b, ee), True)
+            wsem.append("w_c")
+        if nm == "wc2":
+            need("g", g, allw)
+            send(b, "wq", 896, "wq", 256, 384, "w_c2", pick(b, ee), True)
+            wsem.append("w_c2")
+        if nm == "ws":
+            need("g", g, allw)
+            send(b, "wp", 640, "wp", 0, 640, "w_s", pick(b, ee))
+            wsem.append("w_s")
+        if nm == "fc":
+            land("g", g, "a_c", arr["a_c"])
+            send(c, "xm", 128, "xm", 0, 128, "f_c", pick(c, ee), True)
+        if nm == "fs":
+            land("g", g, "a_s", arr["a_s"])
+            send(c, "xmp", 128, "xmp", 0, 128, "f_s", pick(c, ee))
+
+    C = 0.023
+    zi = [0]
+    zfree = {}
+    atok = {}
+    htok = {}
+
+    def mine(*toks):
+        return lambda: need("t", q, [tk[t] for t in toks])
+
+    def here(*sems):
+        return lambda: [land("t", q, s, arr[s]) for s in sems]
+
+    def partner():
+        return here(*wsem)()
+
+    OWN = mine("wa", "wb")
+    UNIT = {1: (384, 128, 0, 128, [OWN, mine("xo")]),
+            2: (256, 128, 0, 0, [OWN, here("o_c", "o_s")]),
+            3: (0, 128, 0, 512, [OWN, here("a_c", "a_s")]),
+            4: (0, 128, 640, 640, [partner, here("a_c", "a_s")]),
+            5: (128, 128, 0, 768, [OWN, here("f_c", "f_s")]),
+            6: (128, 128, 640, 896, [partner, here("f_c", "f_s")]),
+            7: (256, 256, 640, 256, [partner, here("o_c", "o_s")]),
+            9: (384, 128, 640, 384, [partner, mine("xo")]),
+            10: (256, 128, 640, 256, [partner, here("o_c", "o_s")])}
+
+    def first(u, bs):
+        xcol, n, w, hc, deps = UNIT[u]
+        for bb in bs:
+            k = zi[0] % 5
+            zi[0] += 1
+            if k in zfree:
+                need("t", q, [zfree[k]])
+            for d in deps:
+                d()
+            zv = T.z[:, 512 * k:512 * k + n]
+            t = mark("t", q.matmul_mx(zv, ap("wq", w + 128 * bb, 128), ap("wp", w + 128 * bb, 128),
+                                      ap("xm", xcol, n), ap("xmp", xcol, n), True, True))
+            hv = T.h[:, 4 * hc + bb:4 * (hc + n):4]
+            if CFG["acteng"][bb] == "s":
+                need("s", g.scalar, [t])
+                a = mark("s", g.scalar.activation(hv, zv, ActivationFunctionType.Relu, scale=C))
+            else:
+                need("v", V, [t])
+                a = mark("v", V.tensor_scalar(hv, zv, 0.0, C, AluOpType.max, AluOpType.mult))
+            zfree[k] = a
+            atok[u, bb] = a
+        if bs[-1] == 3:
+            need("v", V, [atok[u, bb] for bb in range(4)])
+            htok[u] = quant("hq", hc, "hp", "h", 4 * hc, n)
+
+    def second(bank, hc, n, w, start, stop, us):
+        need("t", q, [htok[u] for u in us] + [tk["w2"]])
+        return mark("t", q.matmul_mx(T.yps[:, 512 * bank:512 * bank + n], ap("wq", w + 512, 128), ap("wp", w + 512, 128),
+                                     ap("hq", hc, n), ap("hp", hc, n), start, stop))
+
+    pe = pick(c, CFG["fwde"])
+    yo = None
+    for st in CFG["ts"].split():
+        if st[0] == "u":
+            u, _, bs = st[1:].partition(".")
+            first(int(u), [int(k) for k in bs] or [0, 1, 2, 3])
+        if st == "A0":
+            second(0, 512, 128, 0, True, False, [3])
+        if st == "A1":
+            yA = second(0, 640, 128, 640, False, True, [4])
+            if CFG["cpA"] == "s":
+                need("s", g.scalar, [yA])
+                cp = mark("s", g.scalar.activation(T.ypart[:], T.yps[:, 0:128], ActivationFunctionType.Copy))
+            else:
+                need("v", V, [yA])
+                cp = mark("v", V.tensor_copy(T.ypart[:], T.yps[:, 0:128]))
+            need("g", g, [cp])
+            send(c, "lpart", 0, "ypart", 0, 128, "r_part", pe)
+        if st == "C0":
+            second(1, 768, 128, 0, True, False, [5])
+        if st == "C1":
+            yC = second(1, 896, 128, 640, False, True, [6])
+        if st == "S":
+            need("v", V, [yC])
+            land("v", V, "r_part", arr["r_part"])
+            su = mark("v", V.tensor_tensor(T.ysum[:], T.yps[:, 512:640], T.lpart[:], AluOpType.add))
+            need("g", g, [su])
+            send(far_out, "lfar", 0, "ysum", 0, 128, "r_far", pick(far_out, CFG["oute"]))
+        if st == "M0":
+            need("t", q, [cp])
+            second(0, 128, 128, 0, True, False, [1])
+        if st == "M1":
+            yM = second(0, 384, 128, 640, False, True, [9])
+        if st == "K0":
+            second(2, 0, 128, 0, True, False, [2])
+        if st == "K1":
+            yH = second(2, 256, 128, 640, False, True, [10])
+        if st == "H0":
+            second(2, 0, 256, 0, True, False, [1, 2])
+        if st == "H1":
+            yH = yM = second(2, 256, 256, 640, False, True, [7])
+        if st == "HC":
+            need("v", V, [yH])
+            ch = mark("v", V.tensor_copy(T.yhome[:], T.yps[:, 1024:1152]))
+            need("g", g, [ch])
+            send(c, "lhome", 0, "yhome", 0, 128, "r_home", pe)
+        if st in ("HA", "HB"):
+            need("v", V, [yM])
+            land("v", V, "r_home", arr["r_home"])
+            m0 = 1152 if st == "HA" else 0
+            yo = mark("v", V.tensor_tensor(T.yown[:], T.yps[:, m0:m0 + 128], T.lhome[:], AluOpType.add))
+
+    need("s", g.scalar, [yo])
+    g.scalar.dma_start(T.y[:, 128 * e:128 * e + 128], T.yown[:]).then_inc(S["st0"], 16)
+    land("y", g.sync, "r_far", arr["r_far"])
+    g.sync.dma_start(T.y[:, 128 * (1 - e):128 * (1 - e) + 128], T.lfar[:]).then_inc(S["st1"], 16)
+    need("g", g, [("t", done["t"]), ("s", done["s"]), ("v", done["v"])])
+    g.wait_ge(S["sent"], sent[0])
+    g.scalar.wait_ge(S["st0"], 16)
+    g.sync.wait_ge(S["st1"], 16)

@@ -1,323 +1,215 @@
 from concourse.bass import DstId, RemoteDMATransfer
 from concourse.mybir import dt, AluOpType, ActivationFunctionType
 
-CFG = dict(wpair="chip", swap=0, fwde="lo", oute="lo", cpA="s", acteng="svsv",
-           ldsync="x' w1 w2 x", ldscalar="", vq="x' w1 w2 x",
-           gs="xc xs wc:hi ws:lo oc os fc fs",
-           ts="u1 u3 A0 u4 u9 A1 u2 M0 u10 K0 M1 u5 K1 HC u6 C0 C1 S HB")
-
-SCRATCH = {
-    "xin": ("sbuf", [128, 1024], "bfloat16"),
-    "w1in": ("sbuf", [128, 2048], "bfloat16"),
-    "w2in": ("sbuf", [128, 512], "bfloat16"),
-    "xs": ("sbuf", [128, 128], "float8_e4m3fn_x4"),
-    "xsp": ("sbuf", [128, 128], "uint8"),
-    "xm": ("sbuf", [128, 512], "float8_e4m3fn_x4"),
-    "xmp": ("sbuf", [128, 512], "uint8"),
-    "wq": ("sbuf", [128, 1280], "float8_e4m3fn_x4"),
-    "wp": ("sbuf", [128, 1280], "uint8"),
-    "h": ("sbuf", [128, 4096], "bfloat16"),
-    "hq": ("sbuf", [128, 1024], "float8_e4m3fn_x4"),
-    "hp": ("sbuf", [128, 1024], "uint8"),
-    "ypart": ("sbuf", [128, 128], "float32"),
-    "ysum": ("sbuf", [128, 128], "float32"),
-    "yhome": ("sbuf", [128, 128], "float32"),
-    "yown": ("sbuf", [128, 128], "float32"),
-    "lpart": ("sbuf", [128, 128], "float32"),
-    "lhome": ("sbuf", [128, 128], "float32"),
-    "lfar": ("sbuf", [128, 128], "float32"),
-    "z": ("psum", [128, 2560], "float32"),
-    "yps": ("psum", [128, 1536], "float32"),
-}
-SEMAPHORES = ["ldx0", "ldx1", "ldwa", "ldwb", "ldw2", "st0", "st1", "vt", "vs", "vv", "sent",
-              "a_c", "a_s", "f_c", "f_s", "o_c", "o_s", "w_c", "w_c2", "w_s", "r_part", "r_home", "r_far"]
+CFG = dict(wpair="chip", acteng="svsv", ld="x' w02 w24 x v2",
+           gs="xc:lo4 xs:lh4 C02:hi C24:hi P04:lo oc os C45:hi P45:hi fc fs", pe="lo", fe="lo",
+           ts="u1 u3 u4 A0 u2 A1 u10 K0 u5 K1 HC u6 C0 u9.01 C1 S u9.23 M0 M1 HB")
+F8, U8, BF, F32 = "float8_e4m3fn_x4", "uint8", "bfloat16", "float32"
+SCRATCH = {n: ("sbuf", [128, w], d) for n, w, d in (
+    ("xin", 1024, BF), ("w1in", 2048, BF), ("w2in", 512, BF), ("h", 4096, BF),
+    ("xs", 128, F8), ("xm", 512, F8), ("wq", 1280, F8), ("hq", 1024, F8),
+    ("xsp", 128, U8), ("xmp", 512, U8), ("wp", 1280, U8), ("hp", 1024, U8),
+    ("ypart", 128, F32), ("ysum", 128, F32), ("yhome", 128, F32), ("yown", 128, F32),
+    ("lpart", 128, F32), ("lhome", 128, F32), ("lfar", 128, F32))}
+SCRATCH["z"] = ("psum", [128, 2560], F32)
+SCRATCH["yps"] = ("psum", [128, 1536], F32)
+SEMAPHORES = ["ldx0", "ldx1", "ldw0", "ldw1", "ldw2", "ldw3", "ldw4", "st0", "st1", "vt", "vs", "vv", "sent",
+              "a_c", "a_s", "f_c", "f_s", "o_c", "o_s", "w_0", "w_1", "w_2", "w_3", "w_4", "r_part", "r_home", "r_far"]
 
 
 def rank_program(g, core, T, topo):
     rank = T.rank_of(core)
     if rank is None:
         return
-    S = T.sem
+    S, V, q = T.sem, g.vector, g.tensor
     e = T.tables["EX"][rank]
 
+    def one(f):
+        return [k for k in T.cores if f(k)][0]
+
     def chipmate(a):
-        return [k for k in T.cores if k != a and topo.host(a) == topo.host(k) and topo.chip(a) == topo.chip(k)][0]
+        return one(lambda k: k != a and topo.host(a) == topo.host(k) and topo.chip(a) == topo.chip(k))
 
     def matemate(a):
-        return [k for k in T.cores if topo.mates(a, k) and topo.die(a) == topo.die(k)][0]
-
-    def across(a):
-        return [k for k in T.cores if topo.host(k) != topo.host(a) and topo.chip(k) == topo.chip(a) and topo.die(k) == topo.die(a)][0]
+        return one(lambda k: topo.mates(a, k) and topo.die(a) == topo.die(k))
 
     wpair, xpair = (chipmate, matemate) if CFG["wpair"] == "chip" else (matemate, chipmate)
     b, c = wpair(core), xpair(core)
-    far = across(core)
-    far_in, far_out = (xpair(far), far) if CFG["swap"] else (far, xpair(far))
+    far_in = one(lambda k: topo.host(k) != topo.host(core) and topo.chip(k) == topo.chip(core) and topo.die(k) == topo.die(core))
+    far_out = xpair(far_in)
 
     def engines(dst):
         m = topo.mask(core, dst)
         return [k for k in range(m.bit_length()) if m >> k & 1]
 
-    lo = engines(far)
-    allc = engines(chipmate(core))
+    lo, allc = engines(far_in), engines(chipmate(core))
     hi = [k for k in allc if k not in lo]
+    SETS = {"": lo, "lo": lo, "hi": hi, "all": allc, "lo4": lo[::2], "lh4": lo[1::2]}
+    arr = {"sent": 0}
 
-    def pick(dst, which):
-        ok = engines(dst)
-        n = len(lo) // 2
-        want = {"lo": lo, "hi": hi, "all": allc, "lo4": lo[:n], "lh4": lo[n:], "hi4": hi[:n], "hh4": hi[n:]}[which or "lo"]
-        return [k for k in want if k in ok] or ok
-
-    def bits(l):
-        return sum(1 << k for k in l)
-
-    def ap(buf, a, n):
-        return T[buf][:, a:a + n]
-
-    def sides(obuf, oc, ibuf, ic, n, code):
-        o, i = ap(obuf, oc, n), ap(ibuf, ic, n)
-        return (o.bitcast(dt.uint8), i.bitcast(dt.uint8)) if code else (o, i)
-
-    sent = [0]
-    arr = {}
-
-    def send(dst, obuf, oc, ibuf, ic, n, sem, eng, code=False):
-        rid, pid = topo.addr(dst, core)
-        o, i = sides(obuf, oc, ibuf, ic, n, code)
-        sent[0] += len(eng)
-        arr[sem] = len(eng)
-        g.remote_dma(out_ap=o, in_ap=i, remote_sem=S[sem], local_sem=S["sent"], pid=pid, routing_id=rid, dma_engine_mask=bits(eng))
-
-    def fused(l):
+    def send(sets, *l):
         trs = []
-        for dst, obuf, oc, ibuf, ic, n, sem, eng, code in l:
+        for (dst, sem, ob, oc, ib, ic, n), es in zip(l, sets.split("+")):
             rid, pid = topo.addr(dst, core)
-            o, i = sides(obuf, oc, ibuf, ic, n, code)
-            sent[0] += len(eng)
+            o, i = T[ob][:, oc:oc + n], T[ib][:, ic:ic + n]
+            if SCRATCH[ob][2] == F8:
+                o, i = o.bitcast(dt.uint8), i.bitcast(dt.uint8)
+            eng = SETS[es]
+            m = sum(1 << k for k in eng)
             arr[sem] = len(eng)
-            trs.append(RemoteDMATransfer(dst_ids=[DstId(rid=rid, pnc=pid)], dma_engine_mask=bits(eng), remote_sem=S[sem], src=i, dst=o))
-        g.remote_dma_fused(trs, local_sem=S["sent"])
+            arr["sent"] += len(eng)
+            if len(l) == 1:
+                g.remote_dma(out_ap=o, in_ap=i, remote_sem=S[sem], local_sem=S["sent"], pid=pid, routing_id=rid, dma_engine_mask=m)
+            else:
+                trs.append(RemoteDMATransfer(dst_ids=[DstId(rid=rid, pnc=pid)], dma_engine_mask=m, remote_sem=S[sem], src=i, dst=o))
+        if trs:
+            g.remote_dma_fused(trs, local_sem=S["sent"])
 
-    V = g.vector
-    q = g.tensor
-    qsem = {"t": "vt", "s": "vs", "v": "vv"}
+    queues = {"t": q, "s": g.scalar, "v": V, "g": g, "y": g.sync}
     done = {"t": 0, "s": 0, "v": 0}
     known = {}
-    seen = {}
+
+    def wait(qn, sem, n):
+        if known.get((qn, sem), 0) < n:
+            queues[qn].wait_ge(S[sem], n)
+            known[qn, sem] = n
 
     def mark(qn, inst):
         done[qn] += 1
-        inst.then_inc(S[qsem[qn]], 1)
+        inst.then_inc(S["v" + qn], 1)
         return (qn, done[qn])
 
-    def need(qn, queue, toks):
-        m = {}
-        for t in toks:
-            m[t[0]] = max(m.get(t[0], 0), t[1])
-        for s, v in m.items():
-            if known.get((qn, s), 0) < v:
-                queue.wait_ge(S[qsem[s]], v)
-                known[qn, s] = v
+    def need(qn, *toks):
+        for s in "tsv":
+            v = max([k for x, k in toks if x == s] + [0])
+            if v:
+                wait(qn, "v" + s, v)
 
-    def land(qn, queue, sem, n):
-        if seen.get((qn, sem), 0) < n:
-            queue.wait_ge(S[sem], n)
-            seen[qn, sem] = n
+    def land(qn, *sems):
+        for s in sems:
+            wait(qn, s, arr[s])
 
     own0, rem0 = 512 * e, 512 * (1 - e)
-    LD = {"x'": ("xin", "x", rem0, 512, "ldx0"), "x": ("xin", "x", own0, 512, "ldx1"),
-          "wa": ("w1in", "w1", 0, 1024, "ldwa"), "wb": ("w1in", "w1", 1024, 1024, "ldwb"),
-          "w1": ("w1in", "w1", 0, 2048, "ldwa"), "w2": ("w2in", "w2", 0, 512, "ldw2")}
-    for queue, names in ((g.sync, CFG["ldsync"]), (g.scalar, CFG["ldscalar"])):
-        for nm in names.split():
-            o, i, c0, n, sm = LD[nm]
-            queue.dma_start(T[o][:, c0:c0 + n], T[i][:, c0:c0 + n]).then_inc(S[sm], 16)
 
     def quant(out, oc, pl, src, sc, n):
-        return mark("v", V.quantize_mx(ap(out, oc, n), ap(pl, oc, n), ap(src, sc, 4 * n)))
+        return mark("v", V.quantize_mx(T[out][:, oc:oc + n], T[pl][:, oc:oc + n], T[src][:, sc:sc + 4 * n]))
 
     tk = {}
-    for nm in CFG["vq"].split():
-        land("v", V, LD[nm][4], 16)
-        if nm == "x'":
-            tk["xr"] = quant("xs", 0, "xsp", "xin", rem0, 128)
-        if nm == "x":
-            tk["xo"] = quant("xm", 384, "xmp", "xin", own0, 128)
-        if nm == "wa":
-            tk["wa"] = quant("wq", 0, "wp", "w1in", 0, 256)
-        if nm == "wb":
-            tk["wb"] = quant("wq", 256, "wp", "w1in", 1024, 256)
-        if nm == "w1":
-            tk["wa"] = tk["wb"] = quant("wq", 0, "wp", "w1in", 0, 512)
-        if nm == "w2":
-            tk["w2"] = quant("wq", 512, "wp", "w2in", 0, 128)
-
+    LD = {"x'": ("xin", "x", rem0, "ldx0", "xs", 0, "xsp"), "x": ("xin", "x", own0, "ldx1", "xm", 384, "xmp"),
+          "v2": ("w2in", "w2", 0, "ldw4", "wq", 512, "wp")}
+    for i in range(4):
+        LD["w%d" % i] = ("w1in", "w1", 512 * i, "ldw%d" % i, "wq", 128 * i, "wp")
+    for ph in (0, 1):
+        for nm in CFG["ld"].split():
+            w = nm[0] == "w"
+            o, i, c0, sm, cb, cc, pb = LD[nm[:2]]
+            n = int(nm[2]) - int(nm[1]) if w else 1
+            if ph == 0:
+                g.sync.dma_start(T[o][:, c0:c0 + 512 * n], T[i][:, c0:c0 + 512 * n]).then_inc(S[sm], 16)
+            else:
+                wait("v", sm, 16)
+                t = quant(cb, cc, pb, o, c0, 128 * n)
+                for k in ([4] if nm == "v2" else range(int(nm[1]), int(nm[2])) if w else [nm]):
+                    tk[k] = t
+    X = {"xc": (far_in, "a_c", "xm", 0, "xs", 0, 128), "xs": (far_in, "a_s", "xmp", 0, "xsp", 0, 128), "ds": (far_out, "f_s", "xmp", 128, "xsp", 0, 128),
+         "oc": (c, "o_c", "xm", 256, "xm", 384, 128), "os": (c, "o_s", "xmp", 256, "xmp", 384, 128),
+         "fc": (c, "f_c", "xm", 128, "xm", 0, 128), "fs": (c, "f_s", "xmp", 128, "xmp", 0, 128)}
     wsem = []
-    allw = [tk["wa"], tk["wb"], tk["w2"]]
-    for nm in CFG["gs"].split():
-        nm, _, ee = nm.partition(":")
-        es = ee.split("+")
-        if nm == "xc":
-            need("g", g, [tk["xr"]])
-            send(far_in, "xm", 0, "xs", 0, 128, "a_c", pick(far_in, ee), True)
-        if nm == "xs":
-            need("g", g, [tk["xr"]])
-            send(far_in, "xmp", 0, "xsp", 0, 128, "a_s", pick(far_in, ee))
-        if nm == "xs2":
-            need("g", g, [tk["xr"]])
-            fused([(far_in, "xmp", 0, "xsp", 0, 128, "a_s", pick(far_in, es[0]), False),
-                   (far_out, "xmp", 128, "xsp", 0, 128, "f_s", pick(far_out, es[1]), False)])
-        if nm == "oc":
-            need("g", g, [tk["xo"]])
-            send(c, "xm", 256, "xm", 384, 128, "o_c", pick(c, ee), True)
-        if nm == "os":
-            need("g", g, [tk["xo"]])
-            send(c, "xmp", 256, "xmp", 384, 128, "o_s", pick(c, ee))
-        if nm == "fxc":
-            need("g", g, [tk["xr"], tk["xo"]])
-            fused([(far_in, "xm", 0, "xs", 0, 128, "a_c", pick(far_in, es[0]), True),
-                   (c, "xm", 256, "xm", 384, 128, "o_c", pick(c, es[1]), True)])
-        if nm in ("fxs", "fx3"):
-            need("g", g, [tk["xr"], tk["xo"]])
-            fused([(far_in, "xmp", 0, "xsp", 0, 128, "a_s", pick(far_in, es[0]), False),
-                   (c, "xmp", 256, "xmp", 384, 128, "o_s", pick(c, es[1]), False)]
-                  + ([(far_out, "xmp", 128, "xsp", 0, 128, "f_s", pick(far_out, es[2]), False)] if nm == "fx3" else []))
-        if nm == "wc":
-            need("g", g, allw)
-            send(b, "wq", 640, "wq", 0, 640, "w_c", pick(b, ee), True)
-            wsem.append("w_c")
-        if nm == "wc1":
-            need("g", g, [tk["wa"]])
-            send(b, "wq", 640, "wq", 0, 256, "w_c", pick(b, ee), True)
-            wsem.append("w_c")
-        if nm == "wc2":
-            need("g", g, allw)
-            send(b, "wq", 896, "wq", 256, 384, "w_c2", pick(b, ee), True)
-            wsem.append("w_c2")
-        if nm == "ws":
-            need("g", g, allw)
-            send(b, "wp", 640, "wp", 0, 640, "w_s", pick(b, ee))
-            wsem.append("w_s")
-        if nm == "fc":
-            land("g", g, "a_c", arr["a_c"])
-            send(c, "xm", 128, "xm", 0, 128, "f_c", pick(c, ee), True)
-        if nm == "fs":
-            land("g", g, "a_s", arr["a_s"])
-            send(c, "xmp", 128, "xmp", 0, 128, "f_s", pick(c, ee))
+    for item in CFG["gs"].split():
+        nms, _, es = item.partition(":")
+        l = []
+        for nm in nms.split("+"):
+            if nm[0] in "CP":
+                i, j = int(nm[1]), int(nm[2])
+                need("g", *[tk[k] for k in range(i, j)])
+                sm, buf = "w_%d" % len(wsem), "wq" if nm[0] == "C" else "wp"
+                l.append((b, sm, buf, 640 + 128 * i, buf, 128 * i, 128 * (j - i)))
+                wsem.append((i, j, sm))
+            else:
+                if nm[0] == "f":
+                    land("g", "a_" + nm[1])
+                else:
+                    need("g", tk["x" if nm[0] == "o" else "x'"])
+                l.append(X[nm])
+        send(es, *l)
 
     C = 0.023
-    zi = [0]
-    zfree = {}
-    atok = {}
-    htok = {}
+    zi, zfree, atok, htok = [0], {}, {}, {}
 
-    def mine(*toks):
-        return lambda: need("t", q, [tk[t] for t in toks])
+    def slice_here(w, k):
+        if w == 0:
+            need("t", tk[k])
+        else:
+            land("t", *[sm for i, j, sm in wsem if i <= k < j])
 
-    def here(*sems):
-        return lambda: [land("t", q, s, arr[s]) for s in sems]
-
-    def partner():
-        return here(*wsem)()
-
-    OWN = mine("wa", "wb")
-    UNIT = {1: (384, 128, 0, 128, [OWN, mine("xo")]),
-            2: (256, 128, 0, 0, [OWN, here("o_c", "o_s")]),
-            3: (0, 128, 0, 512, [OWN, here("a_c", "a_s")]),
-            4: (0, 128, 640, 640, [partner, here("a_c", "a_s")]),
-            5: (128, 128, 0, 768, [OWN, here("f_c", "f_s")]),
-            6: (128, 128, 640, 896, [partner, here("f_c", "f_s")]),
-            7: (256, 256, 640, 256, [partner, here("o_c", "o_s")]),
-            9: (384, 128, 640, 384, [partner, mine("xo")]),
-            10: (256, 128, 640, 256, [partner, here("o_c", "o_s")])}
+    UNIT = {1: (384, 128, 0, 128, ()), 2: (256, 128, 0, 0, ("o_c", "o_s")), 3: (0, 128, 0, 512, ("a_c", "a_s")),
+            4: (0, 128, 640, 640, ("a_c", "a_s")), 5: (128, 128, 0, 768, ("f_c", "f_s")), 6: (128, 128, 640, 896, ("f_c", "f_s")),
+            7: (256, 256, 640, 256, ("o_c", "o_s")), 9: (384, 128, 640, 384, ()), 10: (256, 128, 640, 256, ("o_c", "o_s"))}
 
     def first(u, bs):
-        xcol, n, w, hc, deps = UNIT[u]
+        xc, n, w, hc, sems = UNIT[u]
         for bb in bs:
             k = zi[0] % 5
             zi[0] += 1
-            if k in zfree:
-                need("t", q, [zfree[k]])
-            for d in deps:
-                d()
+            need("t", *([zfree[k]] if k in zfree else []))
+            if xc + n == 512:
+                need("t", tk["x"])
+            slice_here(w, bb)
+            land("t", *sems)
             zv = T.z[:, 512 * k:512 * k + n]
-            t = mark("t", q.matmul_mx(zv, ap("wq", w + 128 * bb, 128), ap("wp", w + 128 * bb, 128),
-                                      ap("xm", xcol, n), ap("xmp", xcol, n), True, True))
+            wc = w + 128 * bb
+            t = mark("t", q.matmul_mx(zv, T.wq[:, wc:wc + 128], T.wp[:, wc:wc + 128], T.xm[:, xc:xc + n], T.xmp[:, xc:xc + n], True, True))
             hv = T.h[:, 4 * hc + bb:4 * (hc + n):4]
-            if CFG["acteng"][bb] == "s":
-                need("s", g.scalar, [t])
-                a = mark("s", g.scalar.activation(hv, zv, ActivationFunctionType.Relu, scale=C))
-            else:
-                need("v", V, [t])
-                a = mark("v", V.tensor_scalar(hv, zv, 0.0, C, AluOpType.max, AluOpType.mult))
-            zfree[k] = a
-            atok[u, bb] = a
+            eng = CFG["acteng"][bb]
+            need(eng, t)
+            zfree[k] = atok[u, bb] = mark(eng, g.scalar.activation(hv, zv, ActivationFunctionType.Relu, scale=C) if eng == "s"
+                                          else V.tensor_scalar(hv, zv, 0.0, C, AluOpType.max, AluOpType.mult))
         if bs[-1] == 3:
-            need("v", V, [atok[u, bb] for bb in range(4)])
+            need("v", *[atok[u, k] for k in range(4)])
             htok[u] = quant("hq", hc, "hp", "h", 4 * hc, n)
 
-    def second(bank, hc, n, w, start, stop, us):
-        need("t", q, [htok[u] for u in us] + [tk["w2"]])
-        return mark("t", q.matmul_mx(T.yps[:, 512 * bank:512 * bank + n], ap("wq", w + 512, 128), ap("wp", w + 512, 128),
-                                     ap("hq", hc, n), ap("hp", hc, n), start, stop))
+    def second(bank, hc, n, w, start, us):
+        slice_here(w, 4)
+        need("t", *[htok[u] for u in us])
+        return mark("t", q.matmul_mx(T.yps[:, 512 * bank:512 * bank + n], T.wq[:, w + 512:w + 640], T.wp[:, w + 512:w + 640],
+                                     T.hq[:, hc:hc + n], T.hp[:, hc:hc + n], start, not start))
 
-    pe = pick(c, CFG["fwde"])
-    yo = None
+    SEC = {"A0": (0, 512, 128, 0, [3]), "A1": (0, 640, 128, 640, [4]), "C0": (1, 768, 128, 0, [5]), "C1": (1, 896, 128, 640, [6]),
+           "M0": (0, 128, 128, 0, [1]), "M1": (0, 384, 128, 640, [9]), "K0": (2, 0, 128, 0, [2]), "K1": (2, 256, 128, 640, [10]),
+           "H0": (2, 0, 256, 0, [1, 2]), "H1": (2, 256, 256, 640, [7])}
+    y = {}
     for st in CFG["ts"].split():
         if st[0] == "u":
             u, _, bs = st[1:].partition(".")
             first(int(u), [int(k) for k in bs] or [0, 1, 2, 3])
-        if st == "A0":
-            second(0, 512, 128, 0, True, False, [3])
+        if st in SEC:
+            if st == "M0":
+                need("t", cp)
+            bk, hc, n, w, us = SEC[st]
+            y[st] = second(bk, hc, n, w, st[1] == "0", us)
         if st == "A1":
-            yA = second(0, 640, 128, 640, False, True, [4])
-            if CFG["cpA"] == "s":
-                need("s", g.scalar, [yA])
-                cp = mark("s", g.scalar.activation(T.ypart[:], T.yps[:, 0:128], ActivationFunctionType.Copy))
-            else:
-                need("v", V, [yA])
-                cp = mark("v", V.tensor_copy(T.ypart[:], T.yps[:, 0:128]))
-            need("g", g, [cp])
-            send(c, "lpart", 0, "ypart", 0, 128, "r_part", pe)
-        if st == "C0":
-            second(1, 768, 128, 0, True, False, [5])
-        if st == "C1":
-            yC = second(1, 896, 128, 640, False, True, [6])
+            need("s", y["A1"])
+            cp = mark("s", g.scalar.activation(T.ypart[:], T.yps[:, 0:128], ActivationFunctionType.Copy))
+            need("g", cp)
+            send(CFG["pe"], (c, "r_part", "lpart", 0, "ypart", 0, 128))
         if st == "S":
-            need("v", V, [yC])
-            land("v", V, "r_part", arr["r_part"])
-            su = mark("v", V.tensor_tensor(T.ysum[:], T.yps[:, 512:640], T.lpart[:], AluOpType.add))
-            need("g", g, [su])
-            send(far_out, "lfar", 0, "ysum", 0, 128, "r_far", pick(far_out, CFG["oute"]))
-        if st == "M0":
-            need("t", q, [cp])
-            second(0, 128, 128, 0, True, False, [1])
-        if st == "M1":
-            yM = second(0, 384, 128, 640, False, True, [9])
-        if st == "K0":
-            second(2, 0, 128, 0, True, False, [2])
-        if st == "K1":
-            yH = second(2, 256, 128, 640, False, True, [10])
-        if st == "H0":
-            second(2, 0, 256, 0, True, False, [1, 2])
-        if st == "H1":
-            yH = yM = second(2, 256, 256, 640, False, True, [7])
+            need("v", y["C1"])
+            land("v", "r_part")
+            need("g", mark("v", V.tensor_tensor(T.ysum[:], T.yps[:, 512:640], T.lpart[:], AluOpType.add)))
+            send(CFG["fe"], (far_out, "r_far", "lfar", 0, "ysum", 0, 128))
         if st == "HC":
-            need("v", V, [yH])
-            ch = mark("v", V.tensor_copy(T.yhome[:], T.yps[:, 1024:1152]))
-            need("g", g, [ch])
-            send(c, "lhome", 0, "yhome", 0, 128, "r_home", pe)
+            need("v", y["H1"] if "H1" in y else y["K1"])
+            need("g", mark("v", V.tensor_copy(T.yhome[:], T.yps[:, 1024:1152])))
+            send(CFG["pe"], (c, "r_home", "lhome", 0, "yhome", 0, 128))
         if st in ("HA", "HB"):
-            need("v", V, [yM])
-            land("v", V, "r_home", arr["r_home"])
             m0 = 1152 if st == "HA" else 0
-            yo = mark("v", V.tensor_tensor(T.yown[:], T.yps[:, m0:m0 + 128], T.lhome[:], AluOpType.add))
-
-    need("s", g.scalar, [yo])
+            need("v", y["H1"] if "H1" in y else y["M1"])
+            land("v", "r_home")
+            need("s", mark("v", V.tensor_tensor(T.yown[:], T.yps[:, m0:m0 + 128], T.lhome[:], AluOpType.add)))
     g.scalar.dma_start(T.y[:, 128 * e:128 * e + 128], T.yown[:]).then_inc(S["st0"], 16)
-    land("y", g.sync, "r_far", arr["r_far"])
-    g.sync.dma_start(T.y[:, 128 * (1 - e):128 * (1 - e) + 128], T.lfar[:]).then_inc(S["st1"], 16)
-    need("g", g, [("t", done["t"]), ("s", done["s"]), ("v", done["v"])])
-    g.wait_ge(S["sent"], sent[0])
-    g.scalar.wait_ge(S["st0"], 16)
-    g.sync.wait_ge(S["st1"], 16)
+    land("y", "r_far")
+    g.sync.dma_start(T.y[:, 128 - 128 * e:256 - 128 * e], T.lfar[:]).then_inc(S["st1"], 16)
+    need("g", *done.items())
+    wait("g", "sent", arr["sent"])
+    wait("s", "st0", 16)
+    wait("y", "st1", 16)

from concourse.bass import DstId, RemoteDMATransfer
from concourse.mybir import dt, AluOpType, ActivationFunctionType

CFG = dict(wpair="chip", acteng="svsv", ld="x' w02 w24 x v2",
           gs="xc:lo4 xs:lh4 C02:hi C24:hi P04:lo oc os C45:hi P45:hi fc fs", pe="lo", fe="lo",
           ts="u1 u3 u4 A0 u2 A1 u10 K0 u5 K1 HC u6 C0 u9.01 C1 S u9.23 M0 M1 HB")
F8, U8, BF, F32 = "float8_e4m3fn_x4", "uint8", "bfloat16", "float32"
SCRATCH = {n: ("sbuf", [128, w], d) for n, w, d in (
    ("xin", 1024, BF), ("w1in", 2048, BF), ("w2in", 512, BF), ("h", 4096, BF),
    ("xs", 128, F8), ("xm", 512, F8), ("wq", 1280, F8), ("hq", 1024, F8),
    ("xsp", 128, U8), ("xmp", 512, U8), ("wp", 1280, U8), ("hp", 1024, U8),
    ("ypart", 128, F32), ("ysum", 128, F32), ("yhome", 128, F32), ("yown", 128, F32),
    ("lpart", 128, F32), ("lhome", 128, F32), ("lfar", 128, F32))}
SCRATCH["z"] = ("psum", [128, 2560], F32)
SCRATCH["yps"] = ("psum", [128, 1536], F32)
SEMAPHORES = ["ldx0", "ldx1", "ldw0", "ldw1", "ldw2", "ldw3", "ldw4", "st0", "st1", "vt", "vs", "vv", "sent",
              "a_c", "a_s", "f_c", "f_s", "o_c", "o_s", "w_0", "w_1", "w_2", "w_3", "w_4", "r_part", "r_home", "r_far"]


def rank_program(g, core, T, topo):
    rank = T.rank_of(core)
    if rank is None:
        return
    S, V, q = T.sem, g.vector, g.tensor
    e = T.tables["EX"][rank]

    def one(f):
        return [k for k in T.cores if f(k)][0]

    def chipmate(a):
        return one(lambda k: k != a and topo.host(a) == topo.host(k) and topo.chip(a) == topo.chip(k))

    def matemate(a):
        return one(lambda k: topo.mates(a, k) and topo.die(a) == topo.die(k))

    wpair, xpair = (chipmate, matemate) if CFG["wpair"] == "chip" else (matemate, chipmate)
    b, c = wpair(core), xpair(core)
    far_in = one(lambda k: topo.host(k) != topo.host(core) and topo.chip(k) == topo.chip(core) and topo.die(k) == topo.die(core))
    far_out = xpair(far_in)

    def engines(dst):
        m = topo.mask(core, dst)
        return [k for k in range(m.bit_length()) if m >> k & 1]

    lo, allc = engines(far_in), engines(chipmate(core))
    hi = [k for k in allc if k not in lo]
    SETS = {"": lo, "lo": lo, "hi": hi, "all": allc, "lo4": lo[::2], "lh4": lo[1::2]}
    arr = {"sent": 0}

    def send(sets, *l):
        trs = []
        for (dst, sem, ob, oc, ib, ic, n), es in zip(l, sets.split("+")):
            rid, pid = topo.addr(dst, core)
            o, i = T[ob][:, oc:oc + n], T[ib][:, ic:ic + n]
            if SCRATCH[ob][2] == F8:
                o, i = o.bitcast(dt.uint8), i.bitcast(dt.uint8)
            eng = SETS[es]
            m = sum(1 << k for k in eng)
            arr[sem] = len(eng)
            arr["sent"] += len(eng)
            if len(l) == 1:
                g.remote_dma(out_ap=o, in_ap=i, remote_sem=S[sem], local_sem=S["sent"], pid=pid, routing_id=rid, dma_engine_mask=m)
            else:
                trs.append(RemoteDMATransfer(dst_ids=[DstId(rid=rid, pnc=pid)], dma_engine_mask=m, remote_sem=S[sem], src=i, dst=o))
        if trs:
            g.remote_dma_fused(trs, local_sem=S["sent"])

    queues = {"t": q, "s": g.scalar, "v": V, "g": g, "y": g.sync}
    done = {"t": 0, "s": 0, "v": 0}
    known = {}

    def wait(qn, sem, n):
        if known.get((qn, sem), 0) < n:
            queues[qn].wait_ge(S[sem], n)
            known[qn, sem] = n

    def mark(qn, inst):
        done[qn] += 1
        inst.then_inc(S["v" + qn], 1)
        return (qn, done[qn])

    def need(qn, *toks):
        for s in "tsv":
            v = max([k for x, k in toks if x == s] + [0])
            if v:
                wait(qn, "v" + s, v)

    def land(qn, *sems):
        for s in sems:
            wait(qn, s, arr[s])

    own0, rem0 = 512 * e, 512 * (1 - e)

    def quant(out, oc, pl, src, sc, n):
        return mark("v", V.quantize_mx(T[out][:, oc:oc + n], T[pl][:, oc:oc + n], T[src][:, sc:sc + 4 * n]))

    tk = {}
    LD = {"x'": ("xin", "x", rem0, "ldx0", "xs", 0, "xsp"), "x": ("xin", "x", own0, "ldx1", "xm", 384, "xmp"),
          "v2": ("w2in", "w2", 0, "ldw4", "wq", 512, "wp")}
    for i in range(4):
        LD["w%d" % i] = ("w1in", "w1", 512 * i, "ldw%d" % i, "wq", 128 * i, "wp")
    for ph in (0, 1):
        for nm in CFG["ld"].split():
            w = nm[0] == "w"
            o, i, c0, sm, cb, cc, pb = LD[nm[:2]]
            n = int(nm[2]) - int(nm[1]) if w else 1
            if ph == 0:
                g.sync.dma_start(T[o][:, c0:c0 + 512 * n], T[i][:, c0:c0 + 512 * n]).then_inc(S[sm], 16)
            else:
                wait("v", sm, 16)
                t = quant(cb, cc, pb, o, c0, 128 * n)
                for k in ([4] if nm == "v2" else range(int(nm[1]), int(nm[2])) if w else [nm]):
                    tk[k] = t
    X = {"xc": (far_in, "a_c", "xm", 0, "xs", 0, 128), "xs": (far_in, "a_s", "xmp", 0, "xsp", 0, 128), "ds": (far_out, "f_s", "xmp", 128, "xsp", 0, 128),
         "oc": (c, "o_c", "xm", 256, "xm", 384, 128), "os": (c, "o_s", "xmp", 256, "xmp", 384, 128),
         "fc": (c, "f_c", "xm", 128, "xm", 0, 128), "fs": (c, "f_s", "xmp", 128, "xmp", 0, 128)}
    wsem = []
    for item in CFG["gs"].split():
        nms, _, es = item.partition(":")
        l = []
        for nm in nms.split("+"):
            if nm[0] in "CP":
                i, j = int(nm[1]), int(nm[2])
                need("g", *[tk[k] for k in range(i, j)])
                sm, buf = "w_%d" % len(wsem), "wq" if nm[0] == "C" else "wp"
                l.append((b, sm, buf, 640 + 128 * i, buf, 128 * i, 128 * (j - i)))
                wsem.append((i, j, sm))
            else:
                if nm[0] == "f":
                    land("g", "a_" + nm[1])
                else:
                    need("g", tk["x" if nm[0] == "o" else "x'"])
                l.append(X[nm])
        send(es, *l)

    C = 0.023
    zi, zfree, atok, htok = [0], {}, {}, {}

    def slice_here(w, k):
        if w == 0:
            need("t", tk[k])
        else:
            land("t", *[sm for i, j, sm in wsem if i <= k < j])

    UNIT = {1: (384, 128, 0, 128, ()), 2: (256, 128, 0, 0, ("o_c", "o_s")), 3: (0, 128, 0, 512, ("a_c", "a_s")),
            4: (0, 128, 640, 640, ("a_c", "a_s")), 5: (128, 128, 0, 768, ("f_c", "f_s")), 6: (128, 128, 640, 896, ("f_c", "f_s")),
            7: (256, 256, 640, 256, ("o_c", "o_s")), 9: (384, 128, 640, 384, ()), 10: (256, 128, 640, 256, ("o_c", "o_s"))}

    def first(u, bs):
        xc, n, w, hc, sems = UNIT[u]
        for bb in bs:
            k = zi[0] % 5
            zi[0] += 1
            need("t", *([zfree[k]] if k in zfree else []))
            if xc + n == 512:
                need("t", tk["x"])
            slice_here(w, bb)
            land("t", *sems)
            zv = T.z[:, 512 * k:512 * k + n]
            wc = w + 128 * bb
            t = mark("t", q.matmul_mx(zv, T.wq[:, wc:wc + 128], T.wp[:, wc:wc + 128], T.xm[:, xc:xc + n], T.xmp[:, xc:xc + n], True, True))
            hv = T.h[:, 4 * hc + bb:4 * (hc + n):4]
            eng = CFG["acteng"][bb]
            need(eng, t)
            zfree[k] = atok[u, bb] = mark(eng, g.scalar.activation(hv, zv, ActivationFunctionType.Relu, scale=C) if eng == "s"
                                          else V.tensor_scalar(hv, zv, 0.0, C, AluOpType.max, AluOpType.mult))
        if bs[-1] == 3:
            need("v", *[atok[u, k] for k in range(4)])
            htok[u] = quant("hq", hc, "hp", "h", 4 * hc, n)

    def second(bank, hc, n, w, start, us):
        slice_here(w, 4)
        need("t", *[htok[u] for u in us])
        return mark("t", q.matmul_mx(T.yps[:, 512 * bank:512 * bank + n], T.wq[:, w + 512:w + 640], T.wp[:, w + 512:w + 640],
                                     T.hq[:, hc:hc + n], T.hp[:, hc:hc + n], start, not start))

    SEC = {"A0": (0, 512, 128, 0, [3]), "A1": (0, 640, 128, 640, [4]), "C0": (1, 768, 128, 0, [5]), "C1": (1, 896, 128, 640, [6]),
           "M0": (0, 128, 128, 0, [1]), "M1": (0, 384, 128, 640, [9]), "K0": (2, 0, 128, 0, [2]), "K1": (2, 256, 128, 640, [10]),
           "H0": (2, 0, 256, 0, [1, 2]), "H1": (2, 256, 256, 640, [7])}
    y = {}
    for st in CFG["ts"].split():
        if st[0] == "u":
            u, _, bs = st[1:].partition(".")
            first(int(u), [int(k) for k in bs] or [0, 1, 2, 3])
        if st in SEC:
            if st == "M0":
                need("t", cp)
            bk, hc, n, w, us = SEC[st]
            y[st] = second(bk, hc, n, w, st[1] == "0", us)
        if st == "A1":
            need("s", y["A1"])
            cp = mark("s", g.scalar.activation(T.ypart[:], T.yps[:, 0:128], ActivationFunctionType.Copy))
            need("g", cp)
            send(CFG["pe"], (c, "r_part", "lpart", 0, "ypart", 0, 128))
        if st == "S":
            need("v", y["C1"])
            land("v", "r_part")
            need("g", mark("v", V.tensor_tensor(T.ysum[:], T.yps[:, 512:640], T.lpart[:], AluOpType.add)))
            send(CFG["fe"], (far_out, "r_far", "lfar", 0, "ysum", 0, 128))
        if st == "HC":
            need("v", y["H1"] if "H1" in y else y["K1"])
            need("g", mark("v", V.tensor_copy(T.yhome[:], T.yps[:, 1024:1152])))
            send(CFG["pe"], (c, "r_home", "lhome", 0, "yhome", 0, 128))
        if st in ("HA", "HB"):
            m0 = 1152 if st == "HA" else 0
            need("v", y["H1"] if "H1" in y else y["M1"])
            land("v", "r_home")
            need("s", mark("v", V.tensor_tensor(T.yown[:], T.yps[:, m0:m0 + 128], T.lhome[:], AluOpType.add)))
    g.scalar.dma_start(T.y[:, 128 * e:128 * e + 128], T.yown[:]).then_inc(S["st0"], 16)
    land("y", "r_far")
    g.sync.dma_start(T.y[:, 128 - 128 * e:256 - 128 * e], T.lfar[:]).then_inc(S["st1"], 16)
    need("g", *done.items())
    wait("g", "sent", arr["sent"])
    wait("s", "st0", 16)
    wait("y", "st1", 16)
